import numpy as np
import ml_dtypes


def mxq(x, axis, fmt="e4m3"):
    dtype, down = {"e4m3": (ml_dtypes.float8_e4m3fn, 7), "e5m2": (ml_dtypes.float8_e5m2, 14)}[fmt]
    v = np.moveaxis(np.asarray(x, np.float32).astype(ml_dtypes.bfloat16).astype(np.float64), axis, -1)
    blocks = v.reshape(v.shape[:-1] + (-1, 32))
    amax = np.abs(blocks).max(-1, keepdims=True)
    byte = np.maximum(np.where(amax > 0, np.frexp(amax)[1] - 1 + 127, 0) - down, 1)
    scale = np.exp2(byte - 127.0)
    codes = (blocks / scale).astype(np.float32).astype(dtype).astype(np.float64)
    return np.moveaxis((codes * scale).reshape(v.shape), -1, axis)


WIDE = False


def mx_kscale(k):
    if not WIDE:
        return np.ones(k)
    levels = np.array([10, -10, 5, -5, 0])
    if k % 512:
        return np.exp2(np.random.permutation(np.resize(levels, k // 32))).repeat(32)
    a = np.empty((k // 512, 16))
    for p in range(k // 512):
        a[p, :8] = np.random.permutation(np.resize(levels, 8))
        for g in range(8):
            far = levels[np.abs(levels - a[p, g]) >= 10]
            a[p, g + 8] = far[np.random.randint(len(far))]
    return np.exp2(a.ravel()).repeat(32)


def f64(x):
    return np.asarray(x).astype(np.float64)


def striped(idx):
    return np.tile(idx.reshape(-1, 16).T, (8, 1)).astype(np.uint16)


def unstriped(offs):
    return offs[:16].T.reshape(-1).astype(np.int64)


def pack_weight(w):
    k, n = w.shape
    w = f64(np.asarray(w, np.float32).astype(ml_dtypes.bfloat16)).reshape(k // 32, 32, n)
    amax = np.abs(w).max(1)
    byte = np.clip(np.where(amax > 0, np.frexp(amax)[1] - 1 + 127 - 7, 1), 1, 254)
    scaled = (w * np.exp2(127.0 - byte)[:, None, :]).reshape(k, n).astype(np.float32)
    words = np.ascontiguousarray(scaled.reshape(k // 512, 128, 4, n).transpose(0, 1, 3, 2)).astype(ml_dtypes.float8_e4m3fn).view(np.uint8)
    return words, np.ascontiguousarray(byte.astype(np.uint8).reshape(k // 512, 16, n))


def unpack_weight(words, scales):
    g, p, n, _ = words.shape
    vals = np.ascontiguousarray(words).view(ml_dtypes.float8_e4m3fn).astype(np.float64) * np.repeat(np.exp2(scales.astype(np.float64) - 127.0), 8, axis=1)[..., None]
    return vals.transpose(0, 1, 3, 2).reshape(g * 512, n)


K, T, S, H, N = 1024, 1024, 512, 512, 256
P = 2 ** 7


def setup_inputs():
    n = np.random.standard_normal
    s = mx_kscale(K)[:, None]
    u = mx_kscale(H)
    packed_w2 = pack_weight(n((H, N)) / np.sqrt(H) / u[:, None])
    return {
        "xT": (n((K, T)) * s).astype(np.float32),
        "w1": (n((K, H)) / np.sqrt(K) / s * u).astype(np.float32),
        "w2_words": packed_w2[0],
        "w2_scales": packed_w2[1],
        "lam": np.tile(np.random.uniform(0.1, 0.9, S), (P, 1)).astype(np.float32),
        "mu": np.tile(np.random.uniform(0.1, 0.9, S), (P, 1)).astype(np.float32),
        "offs": striped(np.random.permutation(T)[:S]),
        "pos1": striped(np.random.permutation(S)),
    }


def reference(xT, w1, w2_words, w2_scales, lam, mu, offs, pos1):
    xq = mxq(f64(xT)[:, unstriped(offs)], 0, "e4m3")
    h = mxq(f64(w1), 0, "e4m3").T @ xq
    z = h * f64(lam)[:1] + h[:, unstriped(pos1)] * f64(mu)[:1]
    return unpack_weight(w2_words, w2_scales).T @ mxq(z, 0, "e4m3")

@@ -1,0 +1,251 @@
+from contextlib import ExitStack
+
+import concourse.mybir as mybir
+from concourse.masks import make_identity
+
+K, T, S, H, N = 1024, 1024, 512, 512, 256
+FLOPS = 2 * K * H * S + 2 * H * N * S
+
+F32 = mybir.dt.float32
+BF16 = mybir.dt.bfloat16
+I32 = mybir.dt.int32
+U32 = mybir.dt.uint32
+U16 = mybir.dt.uint16
+U8 = mybir.dt.uint8
+FP8X4 = mybir.dt.float8_e4m3fn_x4
+COPY = mybir.ActivationFunctionType.Copy
+MULT = mybir.AluOpType.mult
+ADD = mybir.AluOpType.add
+
+P = 128
+PACK = 4
+K_PASS = P * PACK
+X_CHUNKS = [(0, 0, 512, 256), (0, 512, 256, 128), (0, 768, 256, 128), (1, 0, 512, 256), (1, 512, 256, 192), (1, 768, 256, 96)]
+HALF = 256
+W_TAGS = {(0, 0, 0): "wg0", (0, 0, 1): "wg1", (0, 1, 0): "wg2", (0, 1, 1): "wg3", (1, 0, 0): "wg4", (1, 0, 1): "wg5", (1, 1, 0): "wg3", (1, 1, 1): "wg1"}
+
+
+def tile_picked_mixup_none_e_kernel(tc, xT, w1, w2_words, w2_scales, lam, mu, offs, pos1, out):
+    nc = tc.nc
+    with ExitStack() as ctx:
+        keep = ctx.enter_context(tc.tile_pool(name="keep", bufs=1))
+        psum = ctx.enter_context(tc.psum_pool(name="psum", bufs=1))
+
+        def sb(name, shape, dtype, tag=None):
+            return keep.tile(shape, dtype, name=name, tag=tag or name, align_bytes=64)
+
+        def bank(name, tag, shape):
+            return psum.tile(shape, F32, name=name, tag=tag)
+
+        offs_sb = sb("offs_sb", [P, S // 16], U16)
+        pos_sb = sb("pos_sb", [P, S // 16], U16)
+        ident = sb("ident", [P, P], F32)
+        share_rows = sb("share_rows", [P, P], F32)
+        x_scales = sb("x_scales", [P, T], U8)
+        w2_sc = sb("w2_sc", [P, N], U8)
+        w2_cd = sb("w2_cd", [P, N], U32)
+        nc.gpsimd.memset(x_scales[:].bitcast(I32), 0)
+        nc.gpsimd.memset(share_rows[:], 0.0)
+        nc.gpsimd.memset(w2_sc[:].bitcast(I32), 0)
+        make_identity(nc, ident[:])
+
+        x_raw = []
+        for n, (g, c0, w, sw) in enumerate(X_CHUNKS):
+            raw = sb("x_raw%d" % n, [P, PACK, w], F32)
+            nc.sync.dma_start(out=raw[:], in_=xT[g * K_PASS:(g + 1) * K_PASS, c0:c0 + w].rearrange("(p j) w -> p j w", j=PACK))
+            x_raw.append(raw)
+            if n == 1:
+                nc.sync.dma_start(offs_sb[:], offs)
+        w_raw = {}
+
+        def load_w1(hf):
+            for g in range(2):
+                raw = sb("w_raw%d%d" % (hf, g), [P, PACK, HALF], F32)
+                nc.sync.dma_start(out=raw[:], in_=w1[g * K_PASS:(g + 1) * K_PASS, hf * HALF:(hf + 1) * HALF].rearrange("(p j) w -> p j w", j=PACK))
+                w_raw[hf, g] = raw
+
+        load_w1(0)
+        nc.sync.dma_start(pos_sb[:], pos1)
+        nc.sync.dma_start(out=share_rows[0:4, :], in_=lam[0:1, :].rearrange("r (c q) -> (r c) q", q=P))
+        nc.sync.dma_start(out=share_rows[4:8, :], in_=mu[0:1, :].rearrange("r (c q) -> (r c) q", q=P))
+        load_w1(1)
+        nc.sync.dma_start(out=w2_cd[:].bitcast(I32), in_=w2_words[0].rearrange("p n t -> p (n t)").bitcast(I32))
+        for q in range(4):
+            nc.sync.dma_start(out=w2_sc[32 * q:32 * q + 4, :].bitcast(I32), in_=w2_scales[0, 4 * q:4 * q + 4, :].bitcast(I32))
+
+        x_words = [sb("x_words%d" % g, [P, T], U32) for g in range(2)]
+        picked = {}
+        picked_sc = {}
+
+        def pick_words(g, s):
+            picked[g, s] = sb("picked%d%d" % (g, s), [P, HALF], U32)
+            nc.vector.tensor_copy(picked[g, s][:], x_words[g][:].indirect(offs_sb[:, 16 * s:16 * (s + 1)]))
+
+        def pick_scales(s, tag):
+            picked_sc[s] = sb("picked_sc%d" % s, [P, HALF], U8, tag=tag)
+            nc.vector.tensor_copy(picked_sc[s][:], x_scales[:].indirect(offs_sb[:, 16 * s:16 * (s + 1)]))
+
+        for n, (g, c0, w, sw) in enumerate(X_CHUNKS):
+            grouped = sb("x_grouped%d" % n, [P, w, PACK], BF16)
+            src = x_raw[n]
+            if sw > 0:
+                nc.scalar.activation(
+                    grouped[:, 0:sw, :].rearrange("p (c i) t -> p c t i", i=4),
+                    src[:, :, 0:sw].rearrange("p t (c i) -> p c t i", i=4), COPY)
+            if sw < w:
+                nc.vector.tensor_copy(
+                    out=grouped[:, sw:w, :].rearrange("p (c i) t -> p c t i", i=4),
+                    in_=src[:, :, sw:w].rearrange("p t (c i) -> p c t i", i=4))
+            nc.vector.quantize_mx(
+                out=x_words[g][:, c0:c0 + w].bitcast(FP8X4),
+                scales=x_scales[4 * g:P, c0:c0 + w],
+                in_=grouped[:].rearrange("p w t -> p (w t)"))
+            if c0 + w == T and g == 0:
+                for s in range(2):
+                    pick_words(0, s)
+
+        shares = sb("shares", [P, 8], F32)
+        shT = bank("shT", "G3", [P, P])
+        nc.tensor.transpose(shT[:], share_rows[:], ident[:])
+        nc.scalar.copy(shares[:], shT[:, 0:8])
+        h_sb = {}
+        h_ps = {}
+        w_cd = {}
+        w_sc = {}
+        w_gr = {}
+
+        def interleave_w1(hf, g, u, eng):
+            grouped = sb("w_grouped%d%d%d" % (hf, g, u), [P, P, PACK], BF16, tag=W_TAGS[hf, g, u])
+            dst = grouped[:].rearrange("p (m e) t -> p m t e", e=2)
+            src = w_raw[hf, g][:].rearrange("p t (m u e) -> p u m t e", u=2, e=2)[:, u]
+            if eng == "s":
+                nc.scalar.copy(dst, src)
+            else:
+                nc.vector.tensor_copy(out=dst, in_=src)
+            w_gr[hf, g, u] = grouped
+
+        def quantise_w1(hf, g, u):
+            cd = sb("w_cd%d%d%d" % (hf, g, u), [P, P], U32)
+            sc = sb("w_sc%d%d%d" % (hf, g, u), [P, P], U8)
+            nc.vector.quantize_mx(out=cd[:].bitcast(FP8X4), scales=sc[:], in_=w_gr[hf, g, u][:].rearrange("p w t -> p (w t)"))
+            w_cd[hf, g, u] = cd
+            w_sc[hf, g, u] = sc
+
+        def first_product(hf, u, s, acc):
+            for g in range(2):
+                nc.tensor.matmul_mx(
+                    out=acc, lhsT=w_cd[hf, g, u][:].bitcast(FP8X4), lhsT_scale=w_sc[hf, g, u][:],
+                    rhs=picked[g, s][:].bitcast(FP8X4), rhs_scale=picked_sc[s][4 * g:P, :],
+                    start=(g == 0), stop=(g == 1))
+
+        def whole_tile(hf, u):
+            acc = bank("h%d%d" % (hf, u), "H%d" % (2 * hf + u), [P, S])
+            for s in range(2):
+                first_product(hf, u, s, acc[:, s * HALF:(s + 1) * HALF])
+            h_sb[hf, u] = sb("h_sb%d%d" % (hf, u), [P, S], F32)
+            nc.scalar.copy(h_sb[hf, u][:], acc[:])
+
+        def split_tile(hf, u):
+            h_sb[hf, u] = sb("h_sb%d%d" % (hf, u), [P, S], F32)
+            for s in range(2):
+                acc = bank("h%d%d%d" % (hf, u, s), ("G0", "H0")[s], [P, HALF])
+                first_product(hf, u, s, acc[:])
+                nc.scalar.copy(h_sb[hf, u][:, s * HALF:(s + 1) * HALF], acc[:])
+
+        hT = {}
+
+        def turn_own(hf, u):
+            for jt in range(4):
+                if jt not in hT:
+                    hT[jt] = bank("hT%d" % jt, "G%d" % jt, [P, 2, 2, P])
+                nc.tensor.transpose(hT[jt][:, u, hf, :], h_sb[hf, u][:, jt * P:(jt + 1) * P], ident[:])
+
+        gT = {}
+        g_sb = {}
+
+        def gather(hf, u, s):
+            gt = sb("g%d%d%d" % (hf, u, s), [P, HALF], F32)
+            nc.vector.tensor_copy(gt[:], h_sb[hf, u][:].indirect(pos_sb[:, 16 * s:16 * (s + 1)]))
+            g_sb[hf, u, s] = gt
+
+        def turn_gathered(hf, u, s):
+            for a in range(2):
+                jt = 2 * s + a
+                if jt not in gT:
+                    gT[jt] = bank("gT%d" % jt, "H%d" % jt, [P, 2, 2, P])
+                nc.tensor.transpose(gT[jt][:, u, hf, :], g_sb[hf, u, s][:, a * P:(a + 1) * P], ident[:])
+
+        own = {}
+        zT = {}
+        zg = {}
+        z_cd = {}
+        z_sc = {}
+
+        def scale_own(jt):
+            o = sb("own%d" % jt, [P, H], F32)
+            nc.scalar.activation(o[:], hT[jt][:].rearrange("p u h c -> p (u h c)"), COPY, scale=shares[:, jt:jt + 1])
+            own[jt] = o
+
+        def mix(jt):
+            zT[jt] = sb("zT%d" % jt, [P, H], BF16)
+            nc.vector.scalar_tensor_tensor(
+                zT[jt][:], gT[jt][:].rearrange("p u h c -> p (u h c)"), shares[:, 4 + jt:5 + jt], own[jt][:], MULT, ADD)
+
+        def turn_back(jt):
+            zw = bank("zw%d" % jt, "G%d" % jt, [P, 2, P])
+            words = zT[jt][:].bitcast(F32)
+            for u in range(2):
+                nc.tensor.transpose(zw[:, u, :], words[:, u * P:(u + 1) * P], ident[:])
+            z = sb("zg%d" % jt, [P, P * PACK], BF16)
+            nc.scalar.copy(z[:].bitcast(F32).rearrange("p (j u) -> p j u", u=2), zw[:].rearrange("p u j -> p j u"))
+            zg[jt] = z
+
+        def second_product(jt):
+            cd = sb("z_cd%d" % jt, [P, P], U32)
+            sc = sb("z_sc%d" % jt, [P, P], U8)
+            nc.vector.quantize_mx(out=cd[:].bitcast(FP8X4), scales=sc[:], in_=zg[jt][:])
+            acc = bank("o%d" % jt, "H%d" % jt, [P, 2, P])
+            for m in range(2):
+                nc.tensor.matmul_mx(
+                    out=acc[:, m, :], lhsT=w2_cd[:, m * P:(m + 1) * P].bitcast(FP8X4), lhsT_scale=w2_sc[:, m * P:(m + 1) * P],
+                    rhs=cd[:].bitcast(FP8X4), rhs_scale=sc[:], start=True, stop=True)
+            res = sb("res%d" % jt, [P, 2, P], F32)
+            nc.vector.tensor_copy(out=res[:], in_=acc[:])
+            nc.sync.dma_start(out=out[:, jt * P:(jt + 1) * P].rearrange("(m p) j -> p m j", p=P), in_=res[:])
+
+        for g in range(2):
+            for u in range(2):
+                interleave_w1(0, g, u, "s")
+        pick_words(1, 0)
+        pick_scales(0, None)
+        quantise_w1(0, 0, 0)
+        pick_words(1, 1)
+        quantise_w1(0, 1, 0)
+        pick_scales(1, "wg2")
+        split_tile(0, 0)
+        for g in range(2):
+            quantise_w1(0, g, 1)
+        whole_tile(0, 1)
+        for g in range(2):
+            for u in range(2):
+                interleave_w1(1, g, u, "sv"[g])
+        for u in range(2):
+            for g in range(2):
+                quantise_w1(1, g, u)
+            whole_tile(1, u)
+        for hf in range(2):
+            for u in range(2):
+                turn_own(hf, u)
+        for jt in range(4):
+            scale_own(jt)
+        order = [(0, 0, 0), (0, 0, 1), (0, 1, 0), (0, 1, 1), (1, 0, 0), (1, 1, 0), (1, 0, 1), (1, 1, 1)]
+        for key in order:
+            gather(*key)
+        for key in order:
+            turn_gathered(*key)
+        for jt in range(4):
+            mix(jt)
+        for jt in range(4):
+            turn_back(jt)
+        for jt in range(4):
+            second_product(jt)

@@ -20,9 +20,8 @@ ADD = mybir.AluOpType.add
 P = 128
 PACK = 4
 K_PASS = P * PACK
-X_CHUNKS = [(0, 0, 512, 256), (0, 512, 256, 128), (0, 768, 256, 128), (1, 0, 512, 256), (1, 512, 256, 192), (1, 768, 256, 96)]
+X_CHUNKS = [(0, 0, 512, 256), (0, 512, 256, 128), (0, 768, 256, 128), (1, 0, 256, 256), (1, 256, 256, 256), (1, 512, 256, 128), (1, 768, 128, 128), (1, 896, 128, 0)]
 HALF = 256
-W_TAGS = {(0, 0, 0): "wg0", (0, 0, 1): "wg1", (0, 1, 0): "wg2", (0, 1, 1): "wg3", (1, 0, 0): "wg4", (1, 0, 1): "wg5", (1, 1, 0): "wg3", (1, 1, 1): "wg1"}
 
 
 def tile_picked_mixup_none_e_kernel(tc, xT, w1, w2_words, w2_scales, lam, mu, offs, pos1, out):
@@ -56,6 +55,8 @@ def tile_picked_mixup_none_e_kernel(tc, xT, w1, w2_words, w2_scales, lam, mu, of
             x_raw.append(raw)
             if n == 1:
                 nc.sync.dma_start(offs_sb[:], offs)
+                nc.sync.dma_start(out=share_rows[0:4, :], in_=lam[0:1, :].rearrange("r (c q) -> (r c) q", q=P))
+                nc.sync.dma_start(out=share_rows[4:8, :], in_=mu[0:1, :].rearrange("r (c q) -> (r c) q", q=P))
         w_raw = {}
 
         def load_w1(hf):
@@ -66,8 +67,6 @@ def tile_picked_mixup_none_e_kernel(tc, xT, w1, w2_words, w2_scales, lam, mu, of
 
         load_w1(0)
         nc.sync.dma_start(pos_sb[:], pos1)
-        nc.sync.dma_start(out=share_rows[0:4, :], in_=lam[0:1, :].rearrange("r (c q) -> (r c) q", q=P))
-        nc.sync.dma_start(out=share_rows[4:8, :], in_=mu[0:1, :].rearrange("r (c q) -> (r c) q", q=P))
         load_w1(1)
         nc.sync.dma_start(out=w2_cd[:].bitcast(I32), in_=w2_words[0].rearrange("p n t -> p (n t)").bitcast(I32))
         for q in range(4):
@@ -105,7 +104,7 @@ def tile_picked_mixup_none_e_kernel(tc, xT, w1, w2_words, w2_scales, lam, mu, of
                     pick_words(0, s)
 
         shares = sb("shares", [P, 8], F32)
-        shT = bank("shT", "G3", [P, P])
+        shT = bank("shT", "A3", [P, P])
         nc.tensor.transpose(shT[:], share_rows[:], ident[:])
         nc.scalar.copy(shares[:], shT[:, 0:8])
         h_sb = {}
@@ -114,66 +113,58 @@ def tile_picked_mixup_none_e_kernel(tc, xT, w1, w2_words, w2_scales, lam, mu, of
         w_sc = {}
         w_gr = {}
 
-        def interleave_w1(hf, g, u, eng):
-            grouped = sb("w_grouped%d%d%d" % (hf, g, u), [P, P, PACK], BF16, tag=W_TAGS[hf, g, u])
-            dst = grouped[:].rearrange("p (m e) t -> p m t e", e=2)
+        def group_tile(key, width, tag=None):
+            w_gr[key] = sb("w_grouped" + key, [P, width, PACK], BF16, tag=tag)
+            return w_gr[key]
+
+        def interleave_one(hf, g, u, dst):
             src = w_raw[hf, g][:].rearrange("p t (m u e) -> p u m t e", u=2, e=2)[:, u]
-            if eng == "s":
-                nc.scalar.copy(dst, src)
-            else:
-                nc.vector.tensor_copy(out=dst, in_=src)
-            w_gr[hf, g, u] = grouped
+            nc.scalar.copy(dst.rearrange("p (m e) t -> p m t e", e=2), src)
 
-        def quantise_w1(hf, g, u):
-            cd = sb("w_cd%d%d%d" % (hf, g, u), [P, P], U32)
-            sc = sb("w_sc%d%d%d" % (hf, g, u), [P, P], U8)
-            nc.vector.quantize_mx(out=cd[:].bitcast(FP8X4), scales=sc[:], in_=w_gr[hf, g, u][:].rearrange("p w t -> p (w t)"))
-            w_cd[hf, g, u] = cd
-            w_sc[hf, g, u] = sc
+        def interleave_both(hf, g, dst, copy):
+            src = w_raw[hf, g][:].rearrange("p t (m u e) -> p m t u e", u=2, e=2)
+            copy(dst.rearrange("p (u m e) t -> p m t u e", u=2, e=2), src)
 
-        def first_product(hf, u, s, acc):
+        def quantise_w1(key, parts):
+            width = P * len(parts)
+            cd = sb("w_cd" + key, [P, width], U32)
+            sc = sb("w_sc" + key, [P, width], U8)
+            nc.vector.quantize_mx(out=cd[:].bitcast(FP8X4), scales=sc[:], in_=w_gr[key][:].rearrange("p w t -> p (w t)"))
+            for n, part in enumerate(parts):
+                w_cd[part] = cd[:, n * P:(n + 1) * P]
+                w_sc[part] = sc[:, n * P:(n + 1) * P]
+
+        def first_pass(hf, u, g, s, acc):
+            nc.tensor.matmul_mx(
+                out=acc, lhsT=w_cd[hf, g, u].bitcast(FP8X4), lhsT_scale=w_sc[hf, g, u],
+                rhs=picked[g, s][:].bitcast(FP8X4), rhs_scale=picked_sc[s][4 * g:P, :],
+                start=(g == 0), stop=(g == 1))
+
+        def half_product(u, s, acc):
             for g in range(2):
-                nc.tensor.matmul_mx(
-                    out=acc, lhsT=w_cd[hf, g, u][:].bitcast(FP8X4), lhsT_scale=w_sc[hf, g, u][:],
-                    rhs=picked[g, s][:].bitcast(FP8X4), rhs_scale=picked_sc[s][4 * g:P, :],
-                    start=(g == 0), stop=(g == 1))
-
-        def whole_tile(hf, u):
-            acc = bank("h%d%d" % (hf, u), "H%d" % (2 * hf + u), [P, S])
-            for s in range(2):
-                first_product(hf, u, s, acc[:, s * HALF:(s + 1) * HALF])
-            h_sb[hf, u] = sb("h_sb%d%d" % (hf, u), [P, S], F32)
-            nc.scalar.copy(h_sb[hf, u][:], acc[:])
-
-        def split_tile(hf, u):
-            h_sb[hf, u] = sb("h_sb%d%d" % (hf, u), [P, S], F32)
-            for s in range(2):
-                acc = bank("h%d%d%d" % (hf, u, s), ("G0", "H0")[s], [P, HALF])
-                first_product(hf, u, s, acc[:])
-                nc.scalar.copy(h_sb[hf, u][:, s * HALF:(s + 1) * HALF], acc[:])
+                first_pass(0, u, g, s, acc)
 
         hT = {}
 
         def turn_own(hf, u):
             for jt in range(4):
                 if jt not in hT:
-                    hT[jt] = bank("hT%d" % jt, "G%d" % jt, [P, 2, 2, P])
-                nc.tensor.transpose(hT[jt][:, u, hf, :], h_sb[hf, u][:, jt * P:(jt + 1) * P], ident[:])
+                    hT[jt] = bank("hT%d" % jt, "A%d" % jt, [P, 2, 2, P])
+                nc.tensor.transpose(hT[jt][:, u, hf, :], h_sb[hf, u][:, jt * P:(jt + 1) * P], ident_late[:])
 
         gT = {}
         g_sb = {}
+        g_half = {}
 
         def gather(hf, u, s):
-            gt = sb("g%d%d%d" % (hf, u, s), [P, HALF], F32)
-            nc.vector.tensor_copy(gt[:], h_sb[hf, u][:].indirect(pos_sb[:, 16 * s:16 * (s + 1)]))
+            if hf not in g_half:
+                g_half[hf] = sb("g%d" % hf, [P, 2, 2, HALF], F32, tag=("held_by_late", None)[hf])
+            gt = g_half[hf][:, u, s, :]
+            nc.vector.tensor_copy(gt, h_sb[hf, u].indirect(pos_sb[:, 16 * s:16 * (s + 1)]))
             g_sb[hf, u, s] = gt
 
-        def turn_gathered(hf, u, s):
-            for a in range(2):
-                jt = 2 * s + a
-                if jt not in gT:
-                    gT[jt] = bank("gT%d" % jt, "H%d" % jt, [P, 2, 2, P])
-                nc.tensor.transpose(gT[jt][:, u, hf, :], g_sb[hf, u, s][:, a * P:(a + 1) * P], ident[:])
+        def turn_gathered(hf, u, jt):
+            nc.tensor.transpose(gT[jt][:, u, hf, :], g_sb[hf, u, jt // 2][:, (jt % 2) * P:(jt % 2 + 1) * P], ident_late[:])
 
         own = {}
         zT = {}
@@ -192,7 +183,7 @@ def tile_picked_mixup_none_e_kernel(tc, xT, w1, w2_words, w2_scales, lam, mu, of
                 zT[jt][:], gT[jt][:].rearrange("p u h c -> p (u h c)"), shares[:, 4 + jt:5 + jt], own[jt][:], MULT, ADD)
 
         def turn_back(jt):
-            zw = bank("zw%d" % jt, "G%d" % jt, [P, 2, P])
+            zw = bank("zw%d" % jt, "B%d" % jt, [P, 2, P])
             words = zT[jt][:].bitcast(F32)
             for u in range(2):
                 nc.tensor.transpose(zw[:, u, :], words[:, u * P:(u + 1) * P], ident[:])
@@ -204,35 +195,67 @@ def tile_picked_mixup_none_e_kernel(tc, xT, w1, w2_words, w2_scales, lam, mu, of
             cd = sb("z_cd%d" % jt, [P, P], U32)
             sc = sb("z_sc%d" % jt, [P, P], U8)
             nc.vector.quantize_mx(out=cd[:].bitcast(FP8X4), scales=sc[:], in_=zg[jt][:])
-            acc = bank("o%d" % jt, "H%d" % jt, [P, 2, P])
-            for m in range(2):
-                nc.tensor.matmul_mx(
-                    out=acc[:, m, :], lhsT=w2_cd[:, m * P:(m + 1) * P].bitcast(FP8X4), lhsT_scale=w2_sc[:, m * P:(m + 1) * P],
-                    rhs=cd[:].bitcast(FP8X4), rhs_scale=sc[:], start=True, stop=True)
-            res = sb("res%d" % jt, [P, 2, P], F32)
-            nc.vector.tensor_copy(out=res[:], in_=acc[:])
-            nc.sync.dma_start(out=out[:, jt * P:(jt + 1) * P].rearrange("(m p) j -> p m j", p=P), in_=res[:])
+            cols = slice(jt * P, (jt + 1) * P)
 
-        for g in range(2):
-            for u in range(2):
-                interleave_w1(0, g, u, "s")
+            def product(m, acc):
+                nc.tensor.matmul_mx(
+                    out=acc, lhsT=w2_cd[:, m * P:(m + 1) * P].bitcast(FP8X4), lhsT_scale=w2_sc[:, m * P:(m + 1) * P],
+                    rhs=cd[:].bitcast(FP8X4), rhs_scale=sc[:], start=True, stop=True)
+
+            if jt < 3:
+                acc = bank("o%d" % jt, "B%d" % jt, [P, 2, P])
+                for m in range(2):
+                    product(m, acc[:, m, :])
+                res = sb("res%d" % jt, [P, 2, P], F32)
+                (nc.vector.tensor_copy, nc.scalar.copy, nc.scalar.copy)[jt](res[:], acc[:])
+                nc.sync.dma_start(out=out[:, cols].rearrange("(m p) j -> p m j", p=P), in_=res[:])
+            else:
+                for m in range(2):
+                    acc = bank("o3%d" % m, ("A0", "B3")[m], [P, P])
+                    product(m, acc[:])
+                    res = sb("res3%d" % m, [P, P], F32)
+                    (nc.scalar.copy, nc.vector.tensor_copy)[m](res[:], acc[:])
+                    (nc.scalar, nc.sync)[m].dma_start(out=out[m * P:(m + 1) * P, cols], in_=res[:])
+
+        first0 = group_tile("a0", P)
+        first1 = group_tile("a1", P, tag="held_by_scales")
+        second = group_tile("b", 2 * P)
+        interleave_one(0, 0, 0, first0[:])
+        interleave_one(0, 0, 1, second[:, 0:P, :])
+        interleave_one(0, 1, 0, first1[:])
+        interleave_one(0, 1, 1, second[:, P:2 * P, :])
         pick_words(1, 0)
         pick_scales(0, None)
-        quantise_w1(0, 0, 0)
         pick_words(1, 1)
-        quantise_w1(0, 1, 0)
-        pick_scales(1, "wg2")
-        split_tile(0, 0)
-        for g in range(2):
-            quantise_w1(0, g, 1)
-        whole_tile(0, 1)
-        for g in range(2):
+        quantise_w1("a0", [(0, 0, 0)])
+        quantise_w1("a1", [(0, 1, 0)])
+        pick_scales(1, "held_by_scales")
+        quantise_w1("b", [(0, 0, 1), (0, 1, 1)])
+        interleave_both(1, 0, group_tile("c", 2 * P)[:], nc.scalar.copy)
+        interleave_both(1, 1, group_tile("d", 2 * P, tag="held_by_late")[:], nc.vector.tensor_copy)
+        acc_first = [bank("h00%d" % s, "A%d" % s, [P, HALF]) for s in range(2)]
+        acc_second = bank("h01", "A2", [P, S])
+        h_all = sb("h_all", [P, 4, S], F32, tag="w_raw10")
+        for hf in range(2):
             for u in range(2):
-                interleave_w1(1, g, u, "sv"[g])
+                h_sb[hf, u] = h_all[:, 2 * hf + u, :]
+        for s in range(2):
+            half_product(0, s, acc_first[s][:])
+            nc.scalar.copy(h_sb[0, 0][:, s * HALF:(s + 1) * HALF], acc_first[s][:])
+        for s in range(2):
+            half_product(1, s, acc_second[:, s * HALF:(s + 1) * HALF])
+        nc.scalar.copy(h_sb[0, 1], acc_second[:])
+        acc_late = {(u, s): bank("h1%d%d" % (u, s), "B%d" % (2 * u + s), [P, HALF]) for u in range(2) for s in range(2)}
+        for g in range(2):
+            quantise_w1("cd"[g], [(1, g, 0), (1, g, 1)])
+            for u in range(2):
+                for s in range(2):
+                    first_pass(1, u, g, s, acc_late[u, s][:])
         for u in range(2):
-            for g in range(2):
-                quantise_w1(1, g, u)
-            whole_tile(1, u)
+            for s in range(2):
+                nc.scalar.copy(h_sb[1, u][:, s * HALF:(s + 1) * HALF], acc_late[u, s][:])
+        ident_late = sb("ident_late", [P, P], F32, tag="w_raw11")
+        nc.sync.dma_start(out=ident_late[:], in_=ident[:])
         for hf in range(2):
             for u in range(2):
                 turn_own(hf, u)
@@ -241,8 +264,12 @@ def tile_picked_mixup_none_e_kernel(tc, xT, w1, w2_words, w2_scales, lam, mu, of
         order = [(0, 0, 0), (0, 0, 1), (0, 1, 0), (0, 1, 1), (1, 0, 0), (1, 1, 0), (1, 0, 1), (1, 1, 1)]
         for key in order:
             gather(*key)
-        for key in order:
-            turn_gathered(*key)
+        for jt in range(4):
+            gT[jt] = bank("gT%d" % jt, "A%d" % jt, [P, 2, 2, P])
+        for jt in range(4):
+            for hf in range(2):
+                for u in range(2):
+                    turn_gathered(hf, u, jt)
         for jt in range(4):
             mix(jt)
         for jt in range(4):

@@ -89,12 +89,12 @@ def tile_picked_mixup_none_e_kernel(tc, xT, w1, w2_words, w2_scales, lam, mu, of
             src = x_raw[n]
             if sw > 0:
                 nc.scalar.activation(
-                    grouped[:, 0:sw, :].rearrange("p (c i) t -> p c t i", i=4),
-                    src[:, :, 0:sw].rearrange("p t (c i) -> p c t i", i=4), COPY)
+                    grouped[:, 0:sw, :].rearrange("p (c i) t -> p c t i", i=2),
+                    src[:, :, 0:sw].rearrange("p t (c i) -> p c t i", i=2), COPY)
             if sw < w:
                 nc.vector.tensor_copy(
-                    out=grouped[:, sw:w, :].rearrange("p (c i) t -> p c t i", i=4),
-                    in_=src[:, :, sw:w].rearrange("p t (c i) -> p c t i", i=4))
+                    out=grouped[:, sw:w, :].rearrange("p (c i) t -> p c t i", i=2),
+                    in_=src[:, :, sw:w].rearrange("p t (c i) -> p c t i", i=2))
             nc.vector.quantize_mx(
                 out=x_words[g][:, c0:c0 + w].bitcast(FP8X4),
                 scales=x_scales[4 * g:P, c0:c0 + w],
@@ -122,8 +122,8 @@ def tile_picked_mixup_none_e_kernel(tc, xT, w1, w2_words, w2_scales, lam, mu, of
             nc.scalar.copy(dst.rearrange("p (m e) t -> p m t e", e=2), src)
 
         def interleave_both(hf, g, dst, copy):
-            src = w_raw[hf, g][:].rearrange("p t (m u e) -> p m t u e", u=2, e=2)
-            copy(dst.rearrange("p (u m e) t -> p m t u e", u=2, e=2), src)
+            src = w_raw[hf, g][:].rearrange("p t (m u e) -> p u m t e", u=2, e=2)
+            copy(dst.rearrange("p (u m e) t -> p u m t e", u=2, e=2), src)
 
         def quantise_w1(key, parts):
             width = P * len(parts)
@@ -147,7 +147,7 @@ def tile_picked_mixup_none_e_kernel(tc, xT, w1, w2_words, w2_scales, lam, mu, of
         hT = {}
 
         def turn_own(hf, u):
-            for jt in range(4):
+            for jt in range(3):
                 if jt not in hT:
                     hT[jt] = bank("hT%d" % jt, "A%d" % jt, [P, 2, 2, P])
                 nc.tensor.transpose(hT[jt][:, u, hf, :], h_sb[hf, u][:, jt * P:(jt + 1) * P], ident_late[:])
@@ -183,7 +183,7 @@ def tile_picked_mixup_none_e_kernel(tc, xT, w1, w2_words, w2_scales, lam, mu, of
                 zT[jt][:], gT[jt][:].rearrange("p u h c -> p (u h c)"), shares[:, 4 + jt:5 + jt], own[jt][:], MULT, ADD)
 
         def turn_back(jt):
-            zw = bank("zw%d" % jt, "B%d" % jt, [P, 2, P])
+            zw = bank("zw%d" % jt, ("A0", "A1", "A2", "B3")[jt], [P, 2, P])
             words = zT[jt][:].bitcast(F32)
             for u in range(2):
                 nc.tensor.transpose(zw[:, u, :], words[:, u * P:(u + 1) * P], ident[:])
@@ -203,7 +203,7 @@ def tile_picked_mixup_none_e_kernel(tc, xT, w1, w2_words, w2_scales, lam, mu, of
                     rhs=cd[:].bitcast(FP8X4), rhs_scale=sc[:], start=True, stop=True)
 
             if jt < 3:
-                acc = bank("o%d" % jt, "B%d" % jt, [P, 2, P])
+                acc = bank("o%d" % jt, "A%d" % jt, [P, 2, P])
                 for m in range(2):
                     product(m, acc[:, m, :])
                 res = sb("res%d" % jt, [P, 2, P], F32)
@@ -254,18 +254,25 @@ def tile_picked_mixup_none_e_kernel(tc, xT, w1, w2_words, w2_scales, lam, mu, of
         for u in range(2):
             for s in range(2):
                 nc.scalar.copy(h_sb[1, u][:, s * HALF:(s + 1) * HALF], acc_late[u, s][:])
-        ident_late = sb("ident_late", [P, P], F32, tag="w_raw11")
+        ident_late = sb("ident_late", [P, P], F32, tag="w_raw01")
         nc.sync.dma_start(out=ident_late[:], in_=ident[:])
         for hf in range(2):
             for u in range(2):
                 turn_own(hf, u)
+        hT[3] = bank("hT3", "B3", [P, 2, 2, P])
+        for hf in range(2):
+            for u in range(2):
+                for g in range(2):
+                    nc.tensor.matmul_mx(
+                        out=hT[3][:, u, hf, :], lhsT=picked[g, 1][:, P:2 * P].bitcast(FP8X4), lhsT_scale=picked_sc[1][4 * g:P, P:2 * P],
+                        rhs=w_cd[hf, g, u].bitcast(FP8X4), rhs_scale=w_sc[hf, g, u], start=(g == 0), stop=(g == 1))
         for jt in range(4):
             scale_own(jt)
         order = [(0, 0, 0), (0, 0, 1), (0, 1, 0), (0, 1, 1), (1, 0, 0), (1, 1, 0), (1, 0, 1), (1, 1, 1)]
         for key in order:
             gather(*key)
         for jt in range(4):
-            gT[jt] = bank("gT%d" % jt, "A%d" % jt, [P, 2, 2, P])
+            gT[jt] = bank("gT%d" % jt, ("B0", "B1", "B2", "A3")[jt], [P, 2, 2, P])
         for jt in range(4):
             for hf in range(2):
                 for u in range(2):

@@ -20,7 +20,8 @@ ADD = mybir.AluOpType.add
 P = 128
 PACK = 4
 K_PASS = P * PACK
-X_CHUNKS = [(0, 0, 512, 256), (0, 512, 256, 128), (0, 768, 256, 128), (1, 0, 256, 256), (1, 256, 256, 256), (1, 512, 256, 128), (1, 768, 128, 128), (1, 896, 128, 0)]
+X_LOADS = [(0, 0, 512), (0, 512, 512), (1, 0, 512), (1, 512, 512)]
+X_CHUNKS = [(0, 0, 512, 256), (1, 512, 256, 0), (1, 768, 256, 192), (2, 0, 256, 256), (2, 256, 256, 64), (3, 512, 256, 0), (3, 768, 256, 192)]
 HALF = 256
 
 
@@ -49,11 +50,11 @@ def tile_picked_mixup_none_e_kernel(tc, xT, w1, w2_words, w2_scales, lam, mu, of
         make_identity(nc, ident[:])
 
         x_raw = []
-        for n, (g, c0, w, sw) in enumerate(X_CHUNKS):
+        for n, (g, c0, w) in enumerate(X_LOADS):
             raw = sb("x_raw%d" % n, [P, PACK, w], F32)
             nc.sync.dma_start(out=raw[:], in_=xT[g * K_PASS:(g + 1) * K_PASS, c0:c0 + w].rearrange("(p j) w -> p j w", j=PACK))
             x_raw.append(raw)
-            if n == 1:
+            if n == 0:
                 nc.sync.dma_start(offs_sb[:], offs)
                 nc.sync.dma_start(out=share_rows[0:4, :], in_=lam[0:1, :].rearrange("r (c q) -> (r c) q", q=P))
                 nc.sync.dma_start(out=share_rows[4:8, :], in_=mu[0:1, :].rearrange("r (c q) -> (r c) q", q=P))
@@ -84,9 +85,10 @@ def tile_picked_mixup_none_e_kernel(tc, xT, w1, w2_words, w2_scales, lam, mu, of
             picked_sc[s] = sb("picked_sc%d" % s, [P, HALF], U8, tag=tag)
             nc.vector.tensor_copy(picked_sc[s][:], x_scales[:].indirect(offs_sb[:, 16 * s:16 * (s + 1)]))
 
-        for n, (g, c0, w, sw) in enumerate(X_CHUNKS):
+        for n, (load, c0, w, sw) in enumerate(X_CHUNKS):
+            g, first, width = X_LOADS[load]
             grouped = sb("x_grouped%d" % n, [P, w, PACK], BF16)
-            src = x_raw[n]
+            src = x_raw[load][:, :, c0 - first:c0 - first + w]
             if sw > 0:
                 nc.scalar.activation(
                     grouped[:, 0:sw, :].rearrange("p (c i) t -> p c t i", i=2),

from contextlib import ExitStack

import concourse.mybir as mybir
from concourse.masks import make_identity

K, T, S, H, N = 1024, 1024, 512, 512, 256
FLOPS = 2 * K * H * S + 2 * H * N * S

F32 = mybir.dt.float32
BF16 = mybir.dt.bfloat16
I32 = mybir.dt.int32
U32 = mybir.dt.uint32
U16 = mybir.dt.uint16
U8 = mybir.dt.uint8
FP8X4 = mybir.dt.float8_e4m3fn_x4
COPY = mybir.ActivationFunctionType.Copy
MULT = mybir.AluOpType.mult
ADD = mybir.AluOpType.add

P = 128
PACK = 4
K_PASS = P * PACK
X_LOADS = [(0, 0, 512), (0, 512, 512), (1, 0, 512), (1, 512, 512)]
X_CHUNKS = [(0, 0, 512, 256), (1, 512, 256, 0), (1, 768, 256, 192), (2, 0, 256, 256), (2, 256, 256, 64), (3, 512, 256, 0), (3, 768, 256, 192)]
HALF = 256


def tile_picked_mixup_none_e_kernel(tc, xT, w1, w2_words, w2_scales, lam, mu, offs, pos1, out):
    nc = tc.nc
    with ExitStack() as ctx:
        keep = ctx.enter_context(tc.tile_pool(name="keep", bufs=1))
        psum = ctx.enter_context(tc.psum_pool(name="psum", bufs=1))

        def sb(name, shape, dtype, tag=None):
            return keep.tile(shape, dtype, name=name, tag=tag or name, align_bytes=64)

        def bank(name, tag, shape):
            return psum.tile(shape, F32, name=name, tag=tag)

        offs_sb = sb("offs_sb", [P, S // 16], U16)
        pos_sb = sb("pos_sb", [P, S // 16], U16)
        ident = sb("ident", [P, P], F32)
        share_rows = sb("share_rows", [P, P], F32)
        x_scales = sb("x_scales", [P, T], U8)
        w2_sc = sb("w2_sc", [P, N], U8)
        w2_cd = sb("w2_cd", [P, N], U32)
        nc.gpsimd.memset(x_scales[:].bitcast(I32), 0)
        nc.gpsimd.memset(share_rows[:], 0.0)
        nc.gpsimd.memset(w2_sc[:].bitcast(I32), 0)
        make_identity(nc, ident[:])

        x_raw = []
        for n, (g, c0, w) in enumerate(X_LOADS):
            raw = sb("x_raw%d" % n, [P, PACK, w], F32)
            nc.sync.dma_start(out=raw[:], in_=xT[g * K_PASS:(g + 1) * K_PASS, c0:c0 + w].rearrange("(p j) w -> p j w", j=PACK))
            x_raw.append(raw)
            if n == 0:
                nc.sync.dma_start(offs_sb[:], offs)
                nc.sync.dma_start(out=share_rows[0:4, :], in_=lam[0:1, :].rearrange("r (c q) -> (r c) q", q=P))
                nc.sync.dma_start(out=share_rows[4:8, :], in_=mu[0:1, :].rearrange("r (c q) -> (r c) q", q=P))
        w_raw = {}

        def load_w1(hf):
            for g in range(2):
                raw = sb("w_raw%d%d" % (hf, g), [P, PACK, HALF], F32)
                nc.sync.dma_start(out=raw[:], in_=w1[g * K_PASS:(g + 1) * K_PASS, hf * HALF:(hf + 1) * HALF].rearrange("(p j) w -> p j w", j=PACK))
                w_raw[hf, g] = raw

        load_w1(0)
        nc.sync.dma_start(pos_sb[:], pos1)
        load_w1(1)
        nc.sync.dma_start(out=w2_cd[:].bitcast(I32), in_=w2_words[0].rearrange("p n t -> p (n t)").bitcast(I32))
        for q in range(4):
            nc.sync.dma_start(out=w2_sc[32 * q:32 * q + 4, :].bitcast(I32), in_=w2_scales[0, 4 * q:4 * q + 4, :].bitcast(I32))

        x_words = [sb("x_words%d" % g, [P, T], U32) for g in range(2)]
        picked = {}
        picked_sc = {}

        def pick_words(g, s):
            picked[g, s] = sb("picked%d%d" % (g, s), [P, HALF], U32)
            nc.vector.tensor_copy(picked[g, s][:], x_words[g][:].indirect(offs_sb[:, 16 * s:16 * (s + 1)]))

        def pick_scales(s, tag):
            picked_sc[s] = sb("picked_sc%d" % s, [P, HALF], U8, tag=tag)
            nc.vector.tensor_copy(picked_sc[s][:], x_scales[:].indirect(offs_sb[:, 16 * s:16 * (s + 1)]))

        for n, (load, c0, w, sw) in enumerate(X_CHUNKS):
            g, first, width = X_LOADS[load]
            grouped = sb("x_grouped%d" % n, [P, w, PACK], BF16)
            src = x_raw[load][:, :, c0 - first:c0 - first + w]
            if sw > 0:
                nc.scalar.activation(
                    grouped[:, 0:sw, :].rearrange("p (c i) t -> p c t i", i=2),
                    src[:, :, 0:sw].rearrange("p t (c i) -> p c t i", i=2), COPY)
            if sw < w:
                nc.vector.tensor_copy(
                    out=grouped[:, sw:w, :].rearrange("p (c i) t -> p c t i", i=2),
                    in_=src[:, :, sw:w].rearrange("p t (c i) -> p c t i", i=2))
            nc.vector.quantize_mx(
                out=x_words[g][:, c0:c0 + w].bitcast(FP8X4),
                scales=x_scales[4 * g:P, c0:c0 + w],
                in_=grouped[:].rearrange("p w t -> p (w t)"))
            if c0 + w == T and g == 0:
                for s in range(2):
                    pick_words(0, s)

        shares = sb("shares", [P, 8], F32)
        shT = bank("shT", "A3", [P, P])
        nc.tensor.transpose(shT[:], share_rows[:], ident[:])
        nc.scalar.copy(shares[:], shT[:, 0:8])
        h_sb = {}
        h_ps = {}
        w_cd = {}
        w_sc = {}
        w_gr = {}

        def group_tile(key, width, tag=None):
            w_gr[key] = sb("w_grouped" + key, [P, width, PACK], BF16, tag=tag)
            return w_gr[key]

        def interleave_one(hf, g, u, dst):
            src = w_raw[hf, g][:].rearrange("p t (m u e) -> p u m t e", u=2, e=2)[:, u]
            nc.scalar.copy(dst.rearrange("p (m e) t -> p m t e", e=2), src)

        def interleave_both(hf, g, dst, copy):
            src = w_raw[hf, g][:].rearrange("p t (m u e) -> p u m t e", u=2, e=2)
            copy(dst.rearrange("p (u m e) t -> p u m t e", u=2, e=2), src)

        def quantise_w1(key, parts):
            width = P * len(parts)
            cd = sb("w_cd" + key, [P, width], U32)
            sc = sb("w_sc" + key, [P, width], U8)
            nc.vector.quantize_mx(out=cd[:].bitcast(FP8X4), scales=sc[:], in_=w_gr[key][:].rearrange("p w t -> p (w t)"))
            for n, part in enumerate(parts):
                w_cd[part] = cd[:, n * P:(n + 1) * P]
                w_sc[part] = sc[:, n * P:(n + 1) * P]

        def first_pass(hf, u, g, s, acc):
            nc.tensor.matmul_mx(
                out=acc, lhsT=w_cd[hf, g, u].bitcast(FP8X4), lhsT_scale=w_sc[hf, g, u],
                rhs=picked[g, s][:].bitcast(FP8X4), rhs_scale=picked_sc[s][4 * g:P, :],
                start=(g == 0), stop=(g == 1))

        def half_product(u, s, acc):
            for g in range(2):
                first_pass(0, u, g, s, acc)

        hT = {}

        def turn_own(hf, u):
            for jt in range(3):
                if jt not in hT:
                    hT[jt] = bank("hT%d" % jt, "A%d" % jt, [P, 2, 2, P])
                nc.tensor.transpose(hT[jt][:, u, hf, :], h_sb[hf, u][:, jt * P:(jt + 1) * P], ident_late[:])

        gT = {}
        g_sb = {}
        g_half = {}

        def gather(hf, u, s):
            if hf not in g_half:
                g_half[hf] = sb("g%d" % hf, [P, 2, 2, HALF], F32, tag=("held_by_late", None)[hf])
            gt = g_half[hf][:, u, s, :]
            nc.vector.tensor_copy(gt, h_sb[hf, u].indirect(pos_sb[:, 16 * s:16 * (s + 1)]))
            g_sb[hf, u, s] = gt

        def turn_gathered(hf, u, jt):
            nc.tensor.transpose(gT[jt][:, u, hf, :], g_sb[hf, u, jt // 2][:, (jt % 2) * P:(jt % 2 + 1) * P], ident_late[:])

        own = {}
        zT = {}
        zg = {}
        z_cd = {}
        z_sc = {}

        def scale_own(jt):
            o = sb("own%d" % jt, [P, H], F32)
            nc.scalar.activation(o[:], hT[jt][:].rearrange("p u h c -> p (u h c)"), COPY, scale=shares[:, jt:jt + 1])
            own[jt] = o

        def mix(jt):
            zT[jt] = sb("zT%d" % jt, [P, H], BF16)
            nc.vector.scalar_tensor_tensor(
                zT[jt][:], gT[jt][:].rearrange("p u h c -> p (u h c)"), shares[:, 4 + jt:5 + jt], own[jt][:], MULT, ADD)

        def turn_back(jt):
            zw = bank("zw%d" % jt, ("A0", "A1", "A2", "B3")[jt], [P, 2, P])
            words = zT[jt][:].bitcast(F32)
            for u in range(2):
                nc.tensor.transpose(zw[:, u, :], words[:, u * P:(u + 1) * P], ident[:])
            z = sb("zg%d" % jt, [P, P * PACK], BF16)
            nc.scalar.copy(z[:].bitcast(F32).rearrange("p (j u) -> p j u", u=2), zw[:].rearrange("p u j -> p j u"))
            zg[jt] = z

        def second_product(jt):
            cd = sb("z_cd%d" % jt, [P, P], U32)
            sc = sb("z_sc%d" % jt, [P, P], U8)
            nc.vector.quantize_mx(out=cd[:].bitcast(FP8X4), scales=sc[:], in_=zg[jt][:])
            cols = slice(jt * P, (jt + 1) * P)

            def product(m, acc):
                nc.tensor.matmul_mx(
                    out=acc, lhsT=w2_cd[:, m * P:(m + 1) * P].bitcast(FP8X4), lhsT_scale=w2_sc[:, m * P:(m + 1) * P],
                    rhs=cd[:].bitcast(FP8X4), rhs_scale=sc[:], start=True, stop=True)

            if jt < 3:
                acc = bank("o%d" % jt, "A%d" % jt, [P, 2, P])
                for m in range(2):
                    product(m, acc[:, m, :])
                res = sb("res%d" % jt, [P, 2, P], F32)
                (nc.vector.tensor_copy, nc.scalar.copy, nc.scalar.copy)[jt](res[:], acc[:])
                nc.sync.dma_start(out=out[:, cols].rearrange("(m p) j -> p m j", p=P), in_=res[:])
            else:
                for m in range(2):
                    acc = bank("o3%d" % m, ("A0", "B3")[m], [P, P])
                    product(m, acc[:])
                    res = sb("res3%d" % m, [P, P], F32)
                    (nc.scalar.copy, nc.vector.tensor_copy)[m](res[:], acc[:])
                    (nc.scalar, nc.sync)[m].dma_start(out=out[m * P:(m + 1) * P, cols], in_=res[:])

        first0 = group_tile("a0", P)
        first1 = group_tile("a1", P, tag="held_by_scales")
        second = group_tile("b", 2 * P)
        interleave_one(0, 0, 0, first0[:])
        interleave_one(0, 0, 1, second[:, 0:P, :])
        interleave_one(0, 1, 0, first1[:])
        interleave_one(0, 1, 1, second[:, P:2 * P, :])
        pick_words(1, 0)
        pick_scales(0, None)
        pick_words(1, 1)
        quantise_w1("a0", [(0, 0, 0)])
        quantise_w1("a1", [(0, 1, 0)])
        pick_scales(1, "held_by_scales")
        quantise_w1("b", [(0, 0, 1), (0, 1, 1)])
        interleave_both(1, 0, group_tile("c", 2 * P)[:], nc.scalar.copy)
        interleave_both(1, 1, group_tile("d", 2 * P, tag="held_by_late")[:], nc.vector.tensor_copy)
        acc_first = [bank("h00%d" % s, "A%d" % s, [P, HALF]) for s in range(2)]
        acc_second = bank("h01", "A2", [P, S])
        h_all = sb("h_all", [P, 4, S], F32, tag="w_raw10")
        for hf in range(2):
            for u in range(2):
                h_sb[hf, u] = h_all[:, 2 * hf + u, :]
        for s in range(2):
            half_product(0, s, acc_first[s][:])
            nc.scalar.copy(h_sb[0, 0][:, s * HALF:(s + 1) * HALF], acc_first[s][:])
        for s in range(2):
            half_product(1, s, acc_second[:, s * HALF:(s + 1) * HALF])
        nc.scalar.copy(h_sb[0, 1], acc_second[:])
        acc_late = {(u, s): bank("h1%d%d" % (u, s), "B%d" % (2 * u + s), [P, HALF]) for u in range(2) for s in range(2)}
        for g in range(2):
            quantise_w1("cd"[g], [(1, g, 0), (1, g, 1)])
            for u in range(2):
                for s in range(2):
                    first_pass(1, u, g, s, acc_late[u, s][:])
        for u in range(2):
            for s in range(2):
                nc.scalar.copy(h_sb[1, u][:, s * HALF:(s + 1) * HALF], acc_late[u, s][:])
        ident_late = sb("ident_late", [P, P], F32, tag="w_raw01")
        nc.sync.dma_start(out=ident_late[:], in_=ident[:])
        for hf in range(2):
            for u in range(2):
                turn_own(hf, u)
        hT[3] = bank("hT3", "B3", [P, 2, 2, P])
        for hf in range(2):
            for u in range(2):
                for g in range(2):
                    nc.tensor.matmul_mx(
                        out=hT[3][:, u, hf, :], lhsT=picked[g, 1][:, P:2 * P].bitcast(FP8X4), lhsT_scale=picked_sc[1][4 * g:P, P:2 * P],
                        rhs=w_cd[hf, g, u].bitcast(FP8X4), rhs_scale=w_sc[hf, g, u], start=(g == 0), stop=(g == 1))
        for jt in range(4):
            scale_own(jt)
        order = [(0, 0, 0), (0, 0, 1), (0, 1, 0), (0, 1, 1), (1, 0, 0), (1, 1, 0), (1, 0, 1), (1, 1, 1)]
        for key in order:
            gather(*key)
        for jt in range(4):
            gT[jt] = bank("gT%d" % jt, ("B0", "B1", "B2", "A3")[jt], [P, 2, 2, P])
        for jt in range(4):
            for hf in range(2):
                for u in range(2):
                    turn_gathered(hf, u, jt)
        for jt in range(4):
            mix(jt)
        for jt in range(4):
            turn_back(jt)
        for jt in range(4):
            second_product(jt)
